import numpy as np
import ml_dtypes


def mxq(x, axis, fmt="e4m3"):
    dtype, down = {"e4m3": (ml_dtypes.float8_e4m3fn, 7), "e5m2": (ml_dtypes.float8_e5m2, 14)}[fmt]
    v = np.moveaxis(np.asarray(x, np.float32).astype(ml_dtypes.bfloat16).astype(np.float64), axis, -1)
    blocks = v.reshape(v.shape[:-1] + (-1, 32))
    amax = np.abs(blocks).max(-1, keepdims=True)
    byte = np.maximum(np.where(amax > 0, np.frexp(amax)[1] - 1 + 127, 0) - down, 1)
    scale = np.exp2(byte - 127.0)
    codes = (blocks / scale).astype(np.float32).astype(dtype).astype(np.float64)
    return np.moveaxis((codes * scale).reshape(v.shape), -1, axis)


WIDE = False


def mx_kscale(k):
    if not WIDE:
        return np.ones(k)
    levels = np.array([10, -10, 5, -5, 0])
    if k % 512:
        return np.exp2(np.random.permutation(np.resize(levels, k // 32))).repeat(32)
    a = np.empty((k // 512, 16))
    for p in range(k // 512):
        a[p, :8] = np.random.permutation(np.resize(levels, 8))
        for g in range(8):
            far = levels[np.abs(levels - a[p, g]) >= 10]
            a[p, g + 8] = far[np.random.randint(len(far))]
    return np.exp2(a.ravel()).repeat(32)


def f64(x):
    return np.asarray(x).astype(np.float64)


E2M1 = np.array([0.0, 0.5, 1.0, 1.5, 2.0, 3.0, 4.0, 6.0, -0.0, -0.5, -1.0, -1.5, -2.0, -3.0, -4.0, -6.0])


def pack_weight(w, fmt):
    k, n = w.shape
    w = f64(np.asarray(w, np.float32).astype(ml_dtypes.bfloat16)).reshape(k // 32, 32, n)
    amax = np.abs(w).max(1)
    if fmt == "e4m3":
        byte = np.frexp(amax)[1] - 1 + 127 - 7
    else:
        mant, ex = np.frexp(amax / 6.0)
        byte = np.where(mant > 0.5, ex, ex - 1) + 127
    byte = np.clip(np.where(amax > 0, byte, 1), 1, 254)
    scaled = (w * np.exp2(127.0 - byte)[:, None, :]).reshape(k, n).astype(np.float32)
    by_word = np.ascontiguousarray(scaled.reshape(k // 512, 128, 4, n).transpose(0, 1, 3, 2))
    if fmt == "e4m3":
        words = by_word.astype(ml_dtypes.float8_e4m3fn).view(np.uint8)
    else:
        c = by_word.astype(ml_dtypes.float4_e2m1fn).view(np.uint8) & 0xF
        words = (c[..., 0::2] | (c[..., 1::2] << 4)).reshape(k // 512, 128, 2 * n)
    return np.ascontiguousarray(words), np.ascontiguousarray(byte.astype(np.uint8).reshape(k // 512, 16, n))


def unpack_weight(words, scales, fmt):
    g, _, n = scales.shape
    words = np.ascontiguousarray(words).reshape(g, 128, n, -1)
    if fmt == "e4m3":
        vals = words.view(ml_dtypes.float8_e4m3fn).astype(np.float64)
    else:
        nib = np.empty((g, 128, n, 4), np.uint8)
        nib[..., 0::2] = words & 0xF
        nib[..., 1::2] = words >> 4
        vals = E2M1[nib]
    vals = vals * np.repeat(np.exp2(scales.astype(np.float64) - 127.0), 8, axis=1)[..., None]
    return vals.transpose(0, 1, 3, 2).reshape(g * 512, n)


def softplus(v):
    return np.log(1.0 + np.exp(v))


def bf(x):
    return np.asarray(x, np.float32).astype(ml_dtypes.bfloat16)


def planes(Y):
    r, m = Y.shape
    b = f64(bf(Y)).reshape(r // 32, 32, m)
    amax = np.abs(b).max(1)
    byte = np.clip(np.where(amax > 0, np.frexp(amax)[1] - 1 + 127 - 7, 1), 1, 254)
    codes = (b * np.exp2(127.0 - byte)[:, None, :]).reshape(r, m).astype(np.float32).astype(ml_dtypes.float8_e4m3fn).view(np.uint8)
    words = codes.reshape(r // 512, 128, 4, m).transpose(0, 1, 3, 2)
    return np.ascontiguousarray(words), np.ascontiguousarray(byte.astype(np.uint8).reshape(r // 512, 16, m))


K, L, T, N = 1024, 1024, 512, 512


def setup_inputs():
    n = np.random.standard_normal
    fk = mx_kscale(K)
    fl = mx_kscale(L)
    xtp = pack_weight(n((K, T)) / fk[:, None], "e2m1")
    wap = pack_weight(n((K, N)) * 1 / np.sqrt(K) * fk[:, None], "e4m3")
    wqp = pack_weight(n((L, N)) * 1 / np.sqrt(L) * fl[:, None], "e2m1")
    vbp = pack_weight(n((K, N)) * 1 / np.sqrt(K) * fk[:, None], "e4m3")
    vap = pack_weight(n((L, N)) * 1 / np.sqrt(L) * fl[:, None], "e2m1")
    return {
        "xt_words": xtp[0],
        "xt_scales": xtp[1],
        "wa_words": wap[0],
        "wa_scales": wap[1],
        "xq": (n((L, T)) / fl[:, None]).astype(np.float32),
        "wq_words": wqp[0],
        "wq_scales": wqp[1],
        "vb_words": vbp[0],
        "vb_scales": vbp[1],
        "va_words": vap[0],
        "va_scales": vap[1],
    }


def reference(xt_words, xt_scales, wa_words, wa_scales, xq, wq_words, wq_scales, vb_words, vb_scales, va_words, va_scales):
    xtu = unpack_weight(xt_words, xt_scales, "e2m1")
    wau = unpack_weight(wa_words, wa_scales, "e4m3")
    wqu = unpack_weight(wq_words, wq_scales, "e2m1")
    vbu = unpack_weight(vb_words, vb_scales, "e4m3")
    vau = unpack_weight(va_words, va_scales, "e2m1")
    a = wau.T @ xtu
    xqq = mxq(f64(xq), 0, "e4m3")
    b = wqu.T @ xqq
    u = vau.T @ xqq
    v = vbu.T @ xtu
    pa = softplus(u)
    pb = softplus(v)
    y = (pa * a + pb * b) / (pa + pb + 0.1)
    words, scales = planes(y)
    return y, words, scales

@@ -1,0 +1,274 @@
+import math
+from contextlib import ExitStack
+
+import concourse.mybir as mybir
+from concourse.masks import make_identity
+
+K, T, N = 1024, 512, 512
+FLOPS = 4 * 2 * K * T * N
+
+F32 = mybir.dt.float32
+BF16 = mybir.dt.bfloat16
+I32 = mybir.dt.int32
+U32 = mybir.dt.uint32
+U8 = mybir.dt.uint8
+FP8X4 = mybir.dt.float8_e4m3fn_x4
+FP4X4 = mybir.dt.float4_e2m1fn_x4
+ACT = mybir.ActivationFunctionType
+ALU = mybir.AluOpType
+
+P = 128
+PACK = 4
+PASSES = 2
+TT = 128
+TILES = T // TT
+EXP_CAP = 2.0 ** 60
+
+
+def tile_mix_precision_weighted_sums_pl_kernel(
+    tc, xt_words, xt_scales, wa_words, wa_scales, xq, wq_words, wq_scales,
+    vb_words, vb_scales, va_words, va_scales, out_0, out_1, out_2,
+):
+    nc = tc.nc
+    with ExitStack() as ctx:
+        sb = ctx.enter_context(tc.tile_pool(name="sb", bufs=1))
+        ps = ctx.enter_context(tc.psum_pool(name="ps", bufs=1))
+        ctx.enter_context(tc.manual_schedule())
+
+        def tiles(name, shape, dtype, count=TILES):
+            return [sb.tile(shape, dtype, name=name + str(k), align_bytes=64) for k in range(count)]
+
+        xt_w = sb.tile([P, PASSES, 2 * T], U8, align_bytes=64)
+        va_w = sb.tile([P, PASSES, 2 * N], U8, align_bytes=64)
+        wq_w = sb.tile([P, PASSES, 2 * N], U8, align_bytes=64)
+        vb_w = sb.tile([P, PASSES, 4 * N], U8, align_bytes=64)
+        wa_w = sb.tile([P, PASSES, 4 * N], U8, align_bytes=64)
+        xt_s = sb.tile([P, PASSES, T], U8, align_bytes=64)
+        va_s = sb.tile([P, PASSES, N], U8, align_bytes=64)
+        wq_s = sb.tile([P, PASSES, N], U8, align_bytes=64)
+        vb_s = sb.tile([P, PASSES, N], U8, align_bytes=64)
+        wa_s = sb.tile([P, PASSES, N], U8, align_bytes=64)
+        raw0 = sb.tile([P, PACK, T], F32, align_bytes=64)
+        raw1 = tiles("raw1_", [P, PACK, TT], F32)
+        grp0 = tiles("grp0_", [P, T // 2, PACK], BF16, 2)
+        grp1 = tiles("grp1_", [P, TT, PACK], BF16)
+        xq_c = tiles("xq_c", [P, T], U32, PASSES)
+        xq_s = tiles("xq_s", [P, T], U8, PASSES)
+        ones = sb.tile([P, 1], F32, align_bytes=64)
+        warm = sb.tile([P, 1], F32, align_bytes=64)
+        ident = sb.tile([P, P], F32, align_bytes=64)
+        eu = tiles("eu", [P, PACK, P], F32)
+        ev = tiles("ev", [P, PACK, P], F32)
+        cu = tiles("cu", [P, PACK, P], F32)
+        cv = tiles("cv", [P, PACK, P], F32)
+        lu = tiles("lu", [P, PACK, P], F32)
+        lv = tiles("lv", [P, PACK, P], F32)
+        pa = tiles("pa", [P, PACK, P], F32)
+        pb = tiles("pb", [P, PACK, P], F32)
+        ta = tiles("ta", [P, PACK, P], F32)
+        tb = tiles("tb", [P, PACK, P], F32)
+        root = tiles("root", [P, PACK, TT], F32)
+        recip = tiles("recip", [P, PACK, TT], F32)
+        y = tiles("y", [P, PACK, TT], F32)
+        y_grp = tiles("y_grp", [P, TT, PACK], BF16)
+        y_c = tiles("y_c", [P, TT], U32)
+        y_s = sb.tile([P, T], U8, align_bytes=64)
+        bank_u = [ps.tile([P, N], F32, name="bank_u" + str(k)) for k in range(TILES)]
+        bank_v = [ps.tile([P, N], F32, name="bank_v" + str(k)) for k in range(TILES)]
+
+        def cols(k):
+            return slice(k * TT, (k + 1) * TT)
+
+        def dealt(bank):
+            return bank[:].rearrange("p (m r) -> p r m", r=PACK)
+
+        def by_r(bank):
+            return bank[:].rearrange("p (r t) -> p r t", r=PACK)
+
+        def load_fp4(tile, words):
+            nc.sync.dma_start(out=tile[:].bitcast(I32), in_=words.rearrange("z p b -> p z b").bitcast(I32))
+
+        def load_fp8(tile, words):
+            nc.sync.dma_start(out=tile[:].bitcast(I32), in_=words.rearrange("z p c r -> p z (c r)").bitcast(I32))
+
+        def load_scales(queue, plane, scales, quadrants):
+            for q in quadrants:
+                queue.dma_start(
+                    out=plane[32 * q : 32 * q + 4, :, :].bitcast(I32),
+                    in_=scales[:, 4 * q : 4 * q + 4, :].rearrange("z r c -> r z c").bitcast(I32),
+                )
+
+        def interleave(copy, dst, src):
+            copy(
+                out=dst.rearrange("p (c i) j -> p c j i", i=4),
+                in_=src.rearrange("p j (c i) -> p c j i", i=4),
+            )
+
+        def quantize(codes, scales, grouped):
+            nc.vector.quantize_mx(out=codes.bitcast(FP8X4), scales=scales, in_=grouped.rearrange("p c j -> p (c j)"))
+
+        def xt_pass(bank, k, z, words, scales):
+            nc.tensor.matmul_mx(
+                out=bank[:],
+                lhsT=xt_w[:, z, 2 * k * TT : 2 * (k + 1) * TT].bitcast(FP4X4),
+                lhsT_scale=xt_s[:, z, cols(k)],
+                rhs=words[:, z, :].bitcast(FP8X4),
+                rhs_scale=scales[:, z, :],
+                start=(z == 0),
+                stop=(z == PASSES - 1),
+            )
+
+        def xq_pass(bank, k, z, words, scales):
+            nc.tensor.matmul_mx(
+                out=bank[:],
+                lhsT=xq_c[z][:, cols(k)].bitcast(FP8X4),
+                lhsT_scale=xq_s[z][:, cols(k)],
+                rhs=words[:, z, :].bitcast(FP4X4),
+                rhs_scale=scales[:, z, :],
+                start=(z == 0),
+                stop=(z == PASSES - 1),
+            )
+
+        def transpose_into(bank, src, first, last):
+            for r in range(PACK):
+                nc.tensor.matmul(
+                    by_r(bank)[:, r, :], src[:, r, :], ident[:],
+                    start=(first and r == 0), stop=(last and r == PACK - 1), is_transpose=True,
+                )
+
+        for plane in (xt_s, vb_s, va_s):
+            nc.vector.memset(plane[:].bitcast(U32), 0)
+        nc.vector.memset(ones[:], 1.0)
+        for plane in (wq_s, wa_s):
+            nc.vector.memset(plane[:].bitcast(U32), 0)
+
+        load_fp4(xt_w, xt_words)
+        load_fp8(vb_w, vb_words)
+        load_scales(nc.scalar, xt_s, xt_scales, range(4))
+        load_scales(nc.scalar, vb_s, vb_scales, range(2))
+        nc.scalar.activation(out=warm[:], in_=ones[:], func=ACT.Exp)
+        make_identity(nc, ident[:])
+        xq_rows = xq.rearrange("(z p j) t -> z p j t", z=PASSES, j=PACK)
+        nc.sync.dma_start(out=raw0[:], in_=xq_rows[0])
+        load_scales(nc.scalar, vb_s, vb_scales, range(2, 4))
+        load_fp4(va_w, va_words)
+        for k in range(2):
+            nc.sync.dma_start(out=raw1[k][:], in_=xq_rows[1][:, :, cols(k)])
+        load_scales(nc.scalar, va_s, va_scales, range(4))
+        for k in range(2, TILES):
+            nc.sync.dma_start(out=raw1[k][:], in_=xq_rows[1][:, :, cols(k)])
+        load_fp4(wq_w, wq_words)
+        load_fp8(wa_w, wa_words)
+        load_scales(nc.sync, wq_s, wq_scales, range(4))
+        load_scales(nc.sync, wa_s, wa_scales, range(4))
+
+        def exp_of(e, bank):
+            nc.scalar.activation(out=e[:], in_=dealt(bank), func=ACT.Exp)
+
+        def cap(c, e):
+            nc.vector.tensor_scalar(out=c[:], in0=e[:], scalar1=EXP_CAP, scalar2=None, op0=ALU.min)
+
+        for k in range(TILES):
+            for z in range(PASSES):
+                xt_pass(bank_v[k], k, z, vb_w, vb_s)
+            exp_of(ev[k], bank_v[k])
+
+        half = T // 2
+        for h in range(2):
+            interleave(nc.vector.tensor_copy, grp0[h][:], raw0[:, :, h * half : (h + 1) * half])
+        for h in range(2):
+            quantize(xq_c[0][:, h * half : (h + 1) * half], xq_s[0][:, h * half : (h + 1) * half], grp0[h][:])
+        for k in range(TILES):
+            xq_pass(bank_u[k], k, 0, va_w, va_s)
+        for k in range(TILES):
+            interleave(nc.vector.tensor_copy, grp1[k][:], raw1[k][:])
+            cap(cv[k], ev[k])
+            quantize(xq_c[1][:, cols(k)], xq_s[1][:, cols(k)], grp1[k][:])
+            xq_pass(bank_u[k], k, 1, va_w, va_s)
+            exp_of(eu[k], bank_u[k])
+        for k in range(TILES):
+            cap(cu[k], eu[k])
+
+        def precisions(k):
+            nc.scalar.activation(out=lv[k][:], in_=cv[k][:], func=ACT.Ln, bias=ones[:])
+            nc.scalar.activation(out=lu[k][:], in_=cu[k][:], func=ACT.Ln, bias=ones[:])
+            nc.vector.tensor_tensor(out=pb[k][:], in0=dealt(bank_v[k]), in1=lv[k][:], op=ALU.max)
+            for z in range(PASSES):
+                xq_pass(bank_v[k], k, z, wq_w, wq_s)
+            nc.vector.tensor_tensor(out=pa[k][:], in0=dealt(bank_u[k]), in1=lu[k][:], op=ALU.max)
+            for z in range(PASSES):
+                xt_pass(bank_u[k], k, z, wa_w, wa_s)
+
+        def products(k):
+            nc.vector.tensor_tensor(out=tb[k][:], in0=dealt(bank_v[k]), in1=pb[k][:], op=ALU.mult)
+            nc.vector.tensor_tensor(out=ta[k][:], in0=dealt(bank_u[k]), in1=pa[k][:], op=ALU.mult)
+
+        def denominator(k):
+            transpose_into(bank_v[k % 2], pa[k], True, False)
+            transpose_into(bank_v[k % 2], pb[k], False, True)
+
+        def numerator(k):
+            transpose_into(bank_u[k], tb[k], True, False)
+            transpose_into(bank_u[k], ta[k], False, True)
+
+        def reciprocal_root(k):
+            nc.scalar.activation(
+                out=root[k][:], in_=by_r(bank_v[k % 2]), func=ACT.Abs_reciprocal_sqrt, scale=10.0, bias=ones[:]
+            )
+
+        def square(k):
+            nc.scalar.activation(out=recip[k][:], in_=root[k][:], func=ACT.Square, scale=math.sqrt(10.0))
+
+        out_rows = out_0.rearrange("(p r) t -> p r t", r=PACK)
+        out_words = out_1[0].rearrange("p c r -> p (c r)").bitcast(I32)
+
+        def result(k):
+            nc.vector.tensor_tensor(out=y[k][:], in0=by_r(bank_u[k]), in1=recip[k][:], op=ALU.mult)
+            nc.sync.dma_start(out=out_rows[:, :, cols(k)], in_=y[k][:])
+
+        def round_result(k):
+            interleave(nc.scalar.copy, y_grp[k][:], y[k][:])
+
+        def planes(k):
+            quantize(y_c[k][:], y_s[:, cols(k)], y_grp[k][:])
+            nc.sync.dma_start(out=out_words[:, cols(k)], in_=y_c[k][:].bitcast(I32))
+
+        precisions(0)
+        precisions(1)
+        products(0)
+        denominator(0)
+        numerator(0)
+        precisions(2)
+        products(1)
+        denominator(1)
+        numerator(1)
+        precisions(3)
+        reciprocal_root(0)
+        square(0)
+        products(2)
+        denominator(2)
+        numerator(2)
+        reciprocal_root(1)
+        square(1)
+        denominator(3)
+        result(0)
+        reciprocal_root(2)
+        square(2)
+        products(3)
+        numerator(3)
+        round_result(0)
+        result(1)
+        reciprocal_root(3)
+        square(3)
+        result(2)
+        round_result(1)
+        planes(0)
+        result(3)
+        round_result(2)
+        round_result(3)
+        for k in range(1, TILES):
+            planes(k)
+        for q in range(4):
+            nc.sync.dma_start(
+                out=out_2[0, 4 * q : 4 * q + 4, :].bitcast(I32), in_=y_s[32 * q : 32 * q + 4, :].bitcast(I32)
+            )

@@ -22,7 +22,8 @@ PACK = 4
 PASSES = 2
 TT = 128
 TILES = T // TT
-EXP_CAP = 2.0 ** 60
+KNEE = 40.0
+EXP_CAP = math.exp(KNEE)
 
 
 def tile_mix_precision_weighted_sums_pl_kernel(
@@ -49,7 +50,8 @@ def tile_mix_precision_weighted_sums_pl_kernel(
         vb_s = sb.tile([P, PASSES, N], U8, align_bytes=64)
         wa_s = sb.tile([P, PASSES, N], U8, align_bytes=64)
         raw0 = sb.tile([P, PACK, T], F32, align_bytes=64)
-        raw1 = tiles("raw1_", [P, PACK, TT], F32)
+        raw1 = tiles("raw1_", [P, PACK, T // 2], F32, 2)
+        both = tiles("both", [P, PACK, P], F32)
         grp0 = tiles("grp0_", [P, T // 2, PACK], BF16, 2)
         grp1 = tiles("grp1_", [P, TT, PACK], BF16)
         xq_c = tiles("xq_c", [P, T], U32, PASSES)
@@ -142,24 +144,22 @@ def tile_mix_precision_weighted_sums_pl_kernel(
         for plane in (wq_s, wa_s):
             nc.vector.memset(plane[:].bitcast(U32), 0)
 
-        load_fp4(xt_w, xt_words)
-        load_fp8(vb_w, vb_words)
-        load_scales(nc.scalar, xt_s, xt_scales, range(4))
-        load_scales(nc.scalar, vb_s, vb_scales, range(2))
         nc.scalar.activation(out=warm[:], in_=ones[:], func=ACT.Exp)
-        make_identity(nc, ident[:])
+        half = T // 2
         xq_rows = xq.rearrange("(z p j) t -> z p j t", z=PASSES, j=PACK)
+        load_fp4(xt_w, xt_words)
+        load_scales(nc.sync, xt_s, xt_scales, range(4))
+        load_fp8(vb_w, vb_words)
+        load_scales(nc.sync, vb_s, vb_scales, range(4))
+        load_scales(nc.gpsimd, va_s, va_scales, range(4))
+        make_identity(nc, ident[:])
         nc.sync.dma_start(out=raw0[:], in_=xq_rows[0])
-        load_scales(nc.scalar, vb_s, vb_scales, range(2, 4))
         load_fp4(va_w, va_words)
-        for k in range(2):
-            nc.sync.dma_start(out=raw1[k][:], in_=xq_rows[1][:, :, cols(k)])
-        load_scales(nc.scalar, va_s, va_scales, range(4))
-        for k in range(2, TILES):
-            nc.sync.dma_start(out=raw1[k][:], in_=xq_rows[1][:, :, cols(k)])
+        nc.sync.dma_start(out=raw1[0][:], in_=xq_rows[1][:, :, :half])
+        nc.sync.dma_start(out=raw1[1][:], in_=xq_rows[1][:, :, half:])
         load_fp4(wq_w, wq_words)
-        load_fp8(wa_w, wa_words)
         load_scales(nc.sync, wq_s, wq_scales, range(4))
+        load_fp8(wa_w, wa_words)
         load_scales(nc.sync, wa_s, wa_scales, range(4))
 
         def exp_of(e, bank):
@@ -168,107 +168,122 @@ def tile_mix_precision_weighted_sums_pl_kernel(
         def cap(c, e):
             nc.vector.tensor_scalar(out=c[:], in0=e[:], scalar1=EXP_CAP, scalar2=None, op0=ALU.min)
 
+        def round_xq1(k):
+            interleave(nc.vector.tensor_copy, grp1[k][:], raw1[k // 2][:, :, cols(k % 2)])
+
+        def finish_u(k):
+            quantize(xq_c[1][:, cols(k)], xq_s[1][:, cols(k)], grp1[k][:])
+            xq_pass(bank_u[k], k, 1, va_w, va_s)
+            exp_of(eu[k], bank_u[k])
+
         for k in range(TILES):
             for z in range(PASSES):
                 xt_pass(bank_v[k], k, z, vb_w, vb_s)
             exp_of(ev[k], bank_v[k])
 
-        half = T // 2
         for h in range(2):
             interleave(nc.vector.tensor_copy, grp0[h][:], raw0[:, :, h * half : (h + 1) * half])
         for h in range(2):
             quantize(xq_c[0][:, h * half : (h + 1) * half], xq_s[0][:, h * half : (h + 1) * half], grp0[h][:])
         for k in range(TILES):
             xq_pass(bank_u[k], k, 0, va_w, va_s)
+        for h in range(2):
+            round_xq1(2 * h)
+            round_xq1(2 * h + 1)
+            finish_u(2 * h)
+            finish_u(2 * h + 1)
         for k in range(TILES):
-            interleave(nc.vector.tensor_copy, grp1[k][:], raw1[k][:])
             cap(cv[k], ev[k])
-            quantize(xq_c[1][:, cols(k)], xq_s[1][:, cols(k)], grp1[k][:])
-            xq_pass(bank_u[k], k, 1, va_w, va_s)
-            exp_of(eu[k], bank_u[k])
         for k in range(TILES):
             cap(cu[k], eu[k])
 
-        def precisions(k):
+        def logs(k):
             nc.scalar.activation(out=lv[k][:], in_=cv[k][:], func=ACT.Ln, bias=ones[:])
             nc.scalar.activation(out=lu[k][:], in_=cu[k][:], func=ACT.Ln, bias=ones[:])
+
+        def precision_b(k):
             nc.vector.tensor_tensor(out=pb[k][:], in0=dealt(bank_v[k]), in1=lv[k][:], op=ALU.max)
-            for z in range(PASSES):
-                xq_pass(bank_v[k], k, z, wq_w, wq_s)
+
+        def precision_a(k):
             nc.vector.tensor_tensor(out=pa[k][:], in0=dealt(bank_u[k]), in1=lu[k][:], op=ALU.max)
             for z in range(PASSES):
                 xt_pass(bank_u[k], k, z, wa_w, wa_s)
+            nc.gpsimd.tensor_tensor(out=both[k][:], in0=pa[k][:], in1=pb[k][:], op=ALU.add)
 
-        def products(k):
-            nc.vector.tensor_tensor(out=tb[k][:], in0=dealt(bank_v[k]), in1=pb[k][:], op=ALU.mult)
+        def product_b(k):
+            nc.vector.tensor_tensor(out=tb[k][:], in0=dealt(bank_u[k]), in1=pb[k][:], op=ALU.mult)
+
+        def product_a(k):
             nc.vector.tensor_tensor(out=ta[k][:], in0=dealt(bank_u[k]), in1=pa[k][:], op=ALU.mult)
 
+        def estimate_b(k):
+            for z in range(PASSES):
+                xq_pass(bank_u[k], k, z, wq_w, wq_s)
+
         def denominator(k):
-            transpose_into(bank_v[k % 2], pa[k], True, False)
-            transpose_into(bank_v[k % 2], pb[k], False, True)
+            transpose_into(bank_v[k], both[k], True, True)
 
         def numerator(k):
-            transpose_into(bank_u[k], tb[k], True, False)
-            transpose_into(bank_u[k], ta[k], False, True)
+            transpose_into(bank_v[k], ta[k], True, False)
+            transpose_into(bank_v[k], tb[k], False, True)
 
         def reciprocal_root(k):
             nc.scalar.activation(
-                out=root[k][:], in_=by_r(bank_v[k % 2]), func=ACT.Abs_reciprocal_sqrt, scale=10.0, bias=ones[:]
+                out=root[k][:], in_=by_r(bank_v[k]), func=ACT.Abs_reciprocal_sqrt, scale=10.0, bias=ones[:]
             )
 
         def square(k):
-            nc.scalar.activation(out=recip[k][:], in_=root[k][:], func=ACT.Square, scale=math.sqrt(10.0))
+            nc.scalar.activation(out=recip[k][:], in_=root[k][:], func=ACT.Square)
 
         out_rows = out_0.rearrange("(p r) t -> p r t", r=PACK)
         out_words = out_1[0].rearrange("p c r -> p (c r)").bitcast(I32)
 
         def result(k):
-            nc.vector.tensor_tensor(out=y[k][:], in0=by_r(bank_u[k]), in1=recip[k][:], op=ALU.mult)
+            nc.vector.scalar_tensor_tensor(
+                out=y[k][:].rearrange("p r t -> p (r t)"), in0=bank_v[k][:], scalar=10.0,
+                in1=recip[k][:].rearrange("p r t -> p (r t)"), op0=ALU.mult, op1=ALU.mult,
+            )
             nc.sync.dma_start(out=out_rows[:, :, cols(k)], in_=y[k][:])
 
         def round_result(k):
-            interleave(nc.scalar.copy, y_grp[k][:], y[k][:])
+            interleave(nc.scalar.copy if k < 3 else nc.vector.tensor_copy, y_grp[k][:], y[k][:])
 
         def planes(k):
             quantize(y_c[k][:], y_s[:, cols(k)], y_grp[k][:])
             nc.sync.dma_start(out=out_words[:, cols(k)], in_=y_c[k][:].bitcast(I32))
 
-        precisions(0)
-        precisions(1)
-        products(0)
-        denominator(0)
-        numerator(0)
-        precisions(2)
-        products(1)
-        denominator(1)
-        numerator(1)
-        precisions(3)
-        reciprocal_root(0)
-        square(0)
-        products(2)
-        denominator(2)
-        numerator(2)
-        reciprocal_root(1)
-        square(1)
-        denominator(3)
+        for k in range(TILES):
+            logs(k)
+        for k in range(TILES):
+            precision_b(k)
+            precision_a(k)
+            if k > 0:
+                denominator(k - 1)
+        for k in range(TILES):
+            product_a(k)
+            estimate_b(k)
+            if k == 0:
+                denominator(TILES - 1)
+        for k in range(TILES):
+            reciprocal_root(k)
+        for k in range(TILES):
+            square(k)
+        for k in range(TILES):
+            product_b(k)
+            numerator(k)
         result(0)
-        reciprocal_root(2)
-        square(2)
-        products(3)
-        numerator(3)
         round_result(0)
         result(1)
-        reciprocal_root(3)
-        square(3)
-        result(2)
         round_result(1)
-        planes(0)
-        result(3)
+        result(2)
         round_result(2)
+        result(3)
+        planes(0)
+        planes(1)
         round_result(3)
-        for k in range(1, TILES):
-            planes(k)
+        planes(2)
+        planes(3)
         for q in range(4):
-            nc.sync.dma_start(
+            nc.scalar.dma_start(
                 out=out_2[0, 4 * q : 4 * q + 4, :].bitcast(I32), in_=y_s[32 * q : 32 * q + 4, :].bitcast(I32)
             )

@@ -1,4 +1,3 @@
-import math
 from contextlib import ExitStack
 
 import concourse.mybir as mybir
@@ -23,7 +22,6 @@ PASSES = 2
 TT = 128
 TILES = T // TT
 KNEE = 40.0
-EXP_CAP = math.exp(KNEE)
 
 
 def tile_mix_precision_weighted_sums_pl_kernel(
@@ -49,9 +47,10 @@ def tile_mix_precision_weighted_sums_pl_kernel(
         wq_s = sb.tile([P, PASSES, N], U8, align_bytes=64)
         vb_s = sb.tile([P, PASSES, N], U8, align_bytes=64)
         wa_s = sb.tile([P, PASSES, N], U8, align_bytes=64)
-        raw0 = sb.tile([P, PACK, T], F32, align_bytes=64)
+        raw0 = tiles("raw0_", [P, PACK, T // 2], F32, 2)
+        u_sb = tiles("u_sb", [P, PACK, P], F32)
         raw1 = tiles("raw1_", [P, PACK, T // 2], F32, 2)
-        both = tiles("both", [P, PACK, P], F32)
+
         grp0 = tiles("grp0_", [P, T // 2, PACK], BF16, 2)
         grp1 = tiles("grp1_", [P, TT, PACK], BF16)
         xq_c = tiles("xq_c", [P, T], U32, PASSES)
@@ -61,8 +60,6 @@ def tile_mix_precision_weighted_sums_pl_kernel(
         ident = sb.tile([P, P], F32, align_bytes=64)
         eu = tiles("eu", [P, PACK, P], F32)
         ev = tiles("ev", [P, PACK, P], F32)
-        cu = tiles("cu", [P, PACK, P], F32)
-        cv = tiles("cv", [P, PACK, P], F32)
         lu = tiles("lu", [P, PACK, P], F32)
         lv = tiles("lv", [P, PACK, P], F32)
         pa = tiles("pa", [P, PACK, P], F32)
@@ -73,7 +70,7 @@ def tile_mix_precision_weighted_sums_pl_kernel(
         recip = tiles("recip", [P, PACK, TT], F32)
         y = tiles("y", [P, PACK, TT], F32)
         y_grp = tiles("y_grp", [P, TT, PACK], BF16)
-        y_c = tiles("y_c", [P, TT], U32)
+        y_c = sb.tile([P, T], U32, align_bytes=64)
         y_s = sb.tile([P, T], U8, align_bytes=64)
         bank_u = [ps.tile([P, N], F32, name="bank_u" + str(k)) for k in range(TILES)]
         bank_v = [ps.tile([P, N], F32, name="bank_v" + str(k)) for k in range(TILES)]
@@ -153,10 +150,11 @@ def tile_mix_precision_weighted_sums_pl_kernel(
         load_scales(nc.sync, vb_s, vb_scales, range(4))
         load_scales(nc.gpsimd, va_s, va_scales, range(4))
         make_identity(nc, ident[:])
-        nc.sync.dma_start(out=raw0[:], in_=xq_rows[0])
-        load_fp4(va_w, va_words)
+        nc.sync.dma_start(out=raw0[0][:], in_=xq_rows[0][:, :, :half])
+        nc.sync.dma_start(out=raw0[1][:], in_=xq_rows[0][:, :, half:])
         nc.sync.dma_start(out=raw1[0][:], in_=xq_rows[1][:, :, :half])
         nc.sync.dma_start(out=raw1[1][:], in_=xq_rows[1][:, :, half:])
+        load_fp4(va_w, va_words)
         load_fp4(wq_w, wq_words)
         load_scales(nc.sync, wq_s, wq_scales, range(4))
         load_fp8(wa_w, wa_words)
@@ -165,67 +163,75 @@ def tile_mix_precision_weighted_sums_pl_kernel(
         def exp_of(e, bank):
             nc.scalar.activation(out=e[:], in_=dealt(bank), func=ACT.Exp)
 
-        def cap(c, e):
-            nc.vector.tensor_scalar(out=c[:], in0=e[:], scalar1=EXP_CAP, scalar2=None, op0=ALU.min)
-
         def round_xq1(k):
             interleave(nc.vector.tensor_copy, grp1[k][:], raw1[k // 2][:, :, cols(k % 2)])
 
-        def finish_u(k):
+        def quantize_xq1(k):
             quantize(xq_c[1][:, cols(k)], xq_s[1][:, cols(k)], grp1[k][:])
-            xq_pass(bank_u[k], k, 1, va_w, va_s)
-            exp_of(eu[k], bank_u[k])
+
+        def log_of(l, c):
+            nc.scalar.activation(out=l[:], in_=c[:], func=ACT.Ln, bias=ones[:])
+
+        def softplus(p, x, l):
+            nc.vector.scalar_tensor_tensor(out=p[:], in0=l[:], scalar=KNEE, in1=x, op0=ALU.min, op1=ALU.max)
+
+        def product(t, bank, p):
+            nc.vector.tensor_tensor(out=t[:], in0=dealt(bank), in1=p[:], op=ALU.mult)
 
         for k in range(TILES):
             for z in range(PASSES):
                 xt_pass(bank_v[k], k, z, vb_w, vb_s)
             exp_of(ev[k], bank_v[k])
 
-        for h in range(2):
-            interleave(nc.vector.tensor_copy, grp0[h][:], raw0[:, :, h * half : (h + 1) * half])
-        for h in range(2):
-            quantize(xq_c[0][:, h * half : (h + 1) * half], xq_s[0][:, h * half : (h + 1) * half], grp0[h][:])
-        for k in range(TILES):
-            xq_pass(bank_u[k], k, 0, va_w, va_s)
-        for h in range(2):
-            round_xq1(2 * h)
-            round_xq1(2 * h + 1)
-            finish_u(2 * h)
-            finish_u(2 * h + 1)
-        for k in range(TILES):
-            cap(cv[k], ev[k])
-        for k in range(TILES):
-            cap(cu[k], eu[k])
+        def round_xq0(h):
+            interleave(nc.vector.tensor_copy, grp0[h][:], raw0[h][:])
 
-        def logs(k):
-            nc.scalar.activation(out=lv[k][:], in_=cv[k][:], func=ACT.Ln, bias=ones[:])
-            nc.scalar.activation(out=lu[k][:], in_=cu[k][:], func=ACT.Ln, bias=ones[:])
+        def quantize_xq0(h):
+            quantize(xq_c[0][:, h * half : (h + 1) * half], xq_s[0][:, h * half : (h + 1) * half], grp0[h][:])
 
         def precision_b(k):
-            nc.vector.tensor_tensor(out=pb[k][:], in0=dealt(bank_v[k]), in1=lv[k][:], op=ALU.max)
+            softplus(pb[k], dealt(bank_v[k]), lv[k])
 
-        def precision_a(k):
-            nc.vector.tensor_tensor(out=pa[k][:], in0=dealt(bank_u[k]), in1=lu[k][:], op=ALU.max)
-            for z in range(PASSES):
-                xt_pass(bank_u[k], k, z, wa_w, wa_s)
-            nc.gpsimd.tensor_tensor(out=both[k][:], in0=pa[k][:], in1=pb[k][:], op=ALU.add)
-
-        def product_b(k):
-            nc.vector.tensor_tensor(out=tb[k][:], in0=dealt(bank_u[k]), in1=pb[k][:], op=ALU.mult)
-
-        def product_a(k):
-            nc.vector.tensor_tensor(out=ta[k][:], in0=dealt(bank_u[k]), in1=pa[k][:], op=ALU.mult)
+        for h in range(2):
+            round_xq0(h)
+            quantize_xq0(h)
+        for k in range(TILES):
+            log_of(lv[k], ev[k])
 
         def estimate_b(k):
+            precision_b(k)
             for z in range(PASSES):
-                xq_pass(bank_u[k], k, z, wq_w, wq_s)
+                xq_pass(bank_v[k], k, z, wq_w, wq_s)
 
-        def denominator(k):
-            transpose_into(bank_v[k], both[k], True, True)
+        for h in range(2):
+            for k in (2 * h, 2 * h + 1):
+                round_xq1(k)
+            for k in (2 * h, 2 * h + 1):
+                quantize_xq1(k)
+        for k in range(TILES):
+            for z in range(PASSES):
+                xq_pass(bank_u[k], k, z, va_w, va_s)
+            exp_of(eu[k], bank_u[k])
+            if k > 0:
+                estimate_b(k - 1)
+        estimate_b(TILES - 1)
+        def product_b(k):
+            product(tb[k], bank_v[k], pb[k])
+            transpose_into(bank_v[k], pb[k], True, False)
 
-        def numerator(k):
-            transpose_into(bank_v[k], ta[k], True, False)
-            transpose_into(bank_v[k], tb[k], False, True)
+        def keep_u(k):
+            nc.vector.tensor_copy(out=u_sb[k][:], in_=dealt(bank_u[k]))
+
+        def estimate_a(k):
+            for z in range(PASSES):
+                xt_pass(bank_u[k], k, z, wa_w, wa_s)
+
+        for k in range(TILES):
+            product_b(k)
+            keep_u(k)
+            if k < 2:
+                estimate_a(k)
+            log_of(lu[k], eu[k])
 
         def reciprocal_root(k):
             nc.scalar.activation(
@@ -233,14 +239,18 @@ def tile_mix_precision_weighted_sums_pl_kernel(
             )
 
         def square(k):
-            nc.scalar.activation(out=recip[k][:], in_=root[k][:], func=ACT.Square)
+            if k < 2:
+                engine = nc.vector if k == 0 else nc.gpsimd
+                engine.tensor_tensor(out=recip[k][:], in0=root[k][:], in1=root[k][:], op=ALU.mult)
+            else:
+                nc.scalar.activation(out=recip[k][:], in_=root[k][:], func=ACT.Square)
 
         out_rows = out_0.rearrange("(p r) t -> p r t", r=PACK)
         out_words = out_1[0].rearrange("p c r -> p (c r)").bitcast(I32)
 
         def result(k):
             nc.vector.scalar_tensor_tensor(
-                out=y[k][:].rearrange("p r t -> p (r t)"), in0=bank_v[k][:], scalar=10.0,
+                out=y[k][:].rearrange("p r t -> p (r t)"), in0=bank_u[k][:], scalar=10.0,
                 in1=recip[k][:].rearrange("p r t -> p (r t)"), op0=ALU.mult, op1=ALU.mult,
             )
             nc.sync.dma_start(out=out_rows[:, :, cols(k)], in_=y[k][:])
@@ -249,40 +259,45 @@ def tile_mix_precision_weighted_sums_pl_kernel(
             interleave(nc.scalar.copy if k < 3 else nc.vector.tensor_copy, y_grp[k][:], y[k][:])
 
         def planes(k):
-            quantize(y_c[k][:], y_s[:, cols(k)], y_grp[k][:])
-            nc.sync.dma_start(out=out_words[:, cols(k)], in_=y_c[k][:].bitcast(I32))
+            quantize(y_c[:, cols(k)], y_s[:, cols(k)], y_grp[k][:])
 
-        for k in range(TILES):
-            logs(k)
-        for k in range(TILES):
-            precision_b(k)
-            precision_a(k)
-            if k > 0:
-                denominator(k - 1)
-        for k in range(TILES):
-            product_a(k)
-            estimate_b(k)
-            if k == 0:
-                denominator(TILES - 1)
+        def store_words(span):
+            nc.sync.dma_start(out=out_words[:, span], in_=y_c[:, span].bitcast(I32))
+
+        def precision_a(k):
+            softplus(pa[k], u_sb[k][:], lu[k])
+            transpose_into(bank_v[k], pa[k], False, True)
+
+        def numerator(k):
+            product(ta[k], bank_u[k], pa[k])
+            transpose_into(bank_u[k], tb[k], True, False)
+            transpose_into(bank_u[k], ta[k], False, True)
+
+        estimate_a(2)
+        precision_a(0)
+        precision_a(1)
+        numerator(0)
+        estimate_a(3)
+        precision_a(2)
+        precision_a(3)
+        numerator(1)
+        numerator(2)
         for k in range(TILES):
             reciprocal_root(k)
         for k in range(TILES):
             square(k)
-        for k in range(TILES):
-            product_b(k)
-            numerator(k)
-        result(0)
-        round_result(0)
-        result(1)
-        round_result(1)
-        result(2)
-        round_result(2)
+        numerator(3)
+        for k in range(TILES - 1):
+            result(k)
+            round_result(k)
         result(3)
         planes(0)
         planes(1)
+        store_words(slice(0, half))
         round_result(3)
         planes(2)
         planes(3)
+        store_words(slice(half, T))
         for q in range(4):
             nc.scalar.dma_start(
                 out=out_2[0, 4 * q : 4 * q + 4, :].bitcast(I32), in_=y_s[32 * q : 32 * q + 4, :].bitcast(I32)

from contextlib import ExitStack

import concourse.mybir as mybir
from concourse.masks import make_identity

K, T, N = 1024, 512, 512
FLOPS = 4 * 2 * K * T * N

F32 = mybir.dt.float32
BF16 = mybir.dt.bfloat16
I32 = mybir.dt.int32
U32 = mybir.dt.uint32
U8 = mybir.dt.uint8
FP8X4 = mybir.dt.float8_e4m3fn_x4
FP4X4 = mybir.dt.float4_e2m1fn_x4
ACT = mybir.ActivationFunctionType
ALU = mybir.AluOpType

P = 128
PACK = 4
PASSES = 2
TT = 128
TILES = T // TT
KNEE = 40.0


def tile_mix_precision_weighted_sums_pl_kernel(
    tc, xt_words, xt_scales, wa_words, wa_scales, xq, wq_words, wq_scales,
    vb_words, vb_scales, va_words, va_scales, out_0, out_1, out_2,
):
    nc = tc.nc
    with ExitStack() as ctx:
        sb = ctx.enter_context(tc.tile_pool(name="sb", bufs=1))
        ps = ctx.enter_context(tc.psum_pool(name="ps", bufs=1))
        ctx.enter_context(tc.manual_schedule())

        def tiles(name, shape, dtype, count=TILES):
            return [sb.tile(shape, dtype, name=name + str(k), align_bytes=64) for k in range(count)]

        xt_w = sb.tile([P, PASSES, 2 * T], U8, align_bytes=64)
        va_w = sb.tile([P, PASSES, 2 * N], U8, align_bytes=64)
        wq_w = sb.tile([P, PASSES, 2 * N], U8, align_bytes=64)
        vb_w = sb.tile([P, PASSES, 4 * N], U8, align_bytes=64)
        wa_w = sb.tile([P, PASSES, 4 * N], U8, align_bytes=64)
        xt_s = sb.tile([P, PASSES, T], U8, align_bytes=64)
        va_s = sb.tile([P, PASSES, N], U8, align_bytes=64)
        wq_s = sb.tile([P, PASSES, N], U8, align_bytes=64)
        vb_s = sb.tile([P, PASSES, N], U8, align_bytes=64)
        wa_s = sb.tile([P, PASSES, N], U8, align_bytes=64)
        raw0 = tiles("raw0_", [P, PACK, T // 2], F32, 2)
        u_sb = tiles("u_sb", [P, PACK, P], F32)
        raw1 = tiles("raw1_", [P, PACK, T // 2], F32, 2)

        grp0 = tiles("grp0_", [P, T // 2, PACK], BF16, 2)
        grp1 = tiles("grp1_", [P, TT, PACK], BF16)
        xq_c = tiles("xq_c", [P, T], U32, PASSES)
        xq_s = tiles("xq_s", [P, T], U8, PASSES)
        ones = sb.tile([P, 1], F32, align_bytes=64)
        warm = sb.tile([P, 1], F32, align_bytes=64)
        ident = sb.tile([P, P], F32, align_bytes=64)
        eu = tiles("eu", [P, PACK, P], F32)
        ev = tiles("ev", [P, PACK, P], F32)
        lu = tiles("lu", [P, PACK, P], F32)
        lv = tiles("lv", [P, PACK, P], F32)
        pa = tiles("pa", [P, PACK, P], F32)
        pb = tiles("pb", [P, PACK, P], F32)
        ta = tiles("ta", [P, PACK, P], F32)
        tb = tiles("tb", [P, PACK, P], F32)
        root = tiles("root", [P, PACK, TT], F32)
        recip = tiles("recip", [P, PACK, TT], F32)
        y = tiles("y", [P, PACK, TT], F32)
        y_grp = tiles("y_grp", [P, TT, PACK], BF16)
        y_c = sb.tile([P, T], U32, align_bytes=64)
        y_s = sb.tile([P, T], U8, align_bytes=64)
        bank_u = [ps.tile([P, N], F32, name="bank_u" + str(k)) for k in range(TILES)]
        bank_v = [ps.tile([P, N], F32, name="bank_v" + str(k)) for k in range(TILES)]

        def cols(k):
            return slice(k * TT, (k + 1) * TT)

        def dealt(bank):
            return bank[:].rearrange("p (m r) -> p r m", r=PACK)

        def by_r(bank):
            return bank[:].rearrange("p (r t) -> p r t", r=PACK)

        def load_fp4(tile, words):
            nc.sync.dma_start(out=tile[:].bitcast(I32), in_=words.rearrange("z p b -> p z b").bitcast(I32))

        def load_fp8(tile, words):
            nc.sync.dma_start(out=tile[:].bitcast(I32), in_=words.rearrange("z p c r -> p z (c r)").bitcast(I32))

        def load_scales(queue, plane, scales, quadrants):
            for q in quadrants:
                queue.dma_start(
                    out=plane[32 * q : 32 * q + 4, :, :].bitcast(I32),
                    in_=scales[:, 4 * q : 4 * q + 4, :].rearrange("z r c -> r z c").bitcast(I32),
                )

        def interleave(copy, dst, src):
            copy(
                out=dst.rearrange("p (c i) j -> p c j i", i=4),
                in_=src.rearrange("p j (c i) -> p c j i", i=4),
            )

        def quantize(codes, scales, grouped):
            nc.vector.quantize_mx(out=codes.bitcast(FP8X4), scales=scales, in_=grouped.rearrange("p c j -> p (c j)"))

        def xt_pass(bank, k, z, words, scales):
            nc.tensor.matmul_mx(
                out=bank[:],
                lhsT=xt_w[:, z, 2 * k * TT : 2 * (k + 1) * TT].bitcast(FP4X4),
                lhsT_scale=xt_s[:, z, cols(k)],
                rhs=words[:, z, :].bitcast(FP8X4),
                rhs_scale=scales[:, z, :],
                start=(z == 0),
                stop=(z == PASSES - 1),
            )

        def xq_pass(bank, k, z, words, scales):
            nc.tensor.matmul_mx(
                out=bank[:],
                lhsT=xq_c[z][:, cols(k)].bitcast(FP8X4),
                lhsT_scale=xq_s[z][:, cols(k)],
                rhs=words[:, z, :].bitcast(FP4X4),
                rhs_scale=scales[:, z, :],
                start=(z == 0),
                stop=(z == PASSES - 1),
            )

        def transpose_into(bank, src, first, last):
            for r in range(PACK):
                nc.tensor.matmul(
                    by_r(bank)[:, r, :], src[:, r, :], ident[:],
                    start=(first and r == 0), stop=(last and r == PACK - 1), is_transpose=True,
                )

        for plane in (xt_s, vb_s, va_s):
            nc.vector.memset(plane[:].bitcast(U32), 0)
        nc.vector.memset(ones[:], 1.0)
        for plane in (wq_s, wa_s):
            nc.vector.memset(plane[:].bitcast(U32), 0)

        nc.scalar.activation(out=warm[:], in_=ones[:], func=ACT.Exp)
        half = T // 2
        xq_rows = xq.rearrange("(z p j) t -> z p j t", z=PASSES, j=PACK)
        load_fp4(xt_w, xt_words)
        load_scales(nc.sync, xt_s, xt_scales, range(4))
        load_fp8(vb_w, vb_words)
        load_scales(nc.sync, vb_s, vb_scales, range(4))
        load_scales(nc.gpsimd, va_s, va_scales, range(4))
        make_identity(nc, ident[:])
        nc.sync.dma_start(out=raw0[0][:], in_=xq_rows[0][:, :, :half])
        nc.sync.dma_start(out=raw0[1][:], in_=xq_rows[0][:, :, half:])
        nc.sync.dma_start(out=raw1[0][:], in_=xq_rows[1][:, :, :half])
        nc.sync.dma_start(out=raw1[1][:], in_=xq_rows[1][:, :, half:])
        load_fp4(va_w, va_words)
        load_fp4(wq_w, wq_words)
        load_scales(nc.sync, wq_s, wq_scales, range(4))
        load_fp8(wa_w, wa_words)
        load_scales(nc.sync, wa_s, wa_scales, range(4))

        def exp_of(e, bank):
            nc.scalar.activation(out=e[:], in_=dealt(bank), func=ACT.Exp)

        def round_xq1(k):
            interleave(nc.vector.tensor_copy, grp1[k][:], raw1[k // 2][:, :, cols(k % 2)])

        def quantize_xq1(k):
            quantize(xq_c[1][:, cols(k)], xq_s[1][:, cols(k)], grp1[k][:])

        def log_of(l, c):
            nc.scalar.activation(out=l[:], in_=c[:], func=ACT.Ln, bias=ones[:])

        def softplus(p, x, l):
            nc.vector.scalar_tensor_tensor(out=p[:], in0=l[:], scalar=KNEE, in1=x, op0=ALU.min, op1=ALU.max)

        def product(t, bank, p):
            nc.vector.tensor_tensor(out=t[:], in0=dealt(bank), in1=p[:], op=ALU.mult)

        for k in range(TILES):
            for z in range(PASSES):
                xt_pass(bank_v[k], k, z, vb_w, vb_s)
            exp_of(ev[k], bank_v[k])

        def round_xq0(h):
            interleave(nc.vector.tensor_copy, grp0[h][:], raw0[h][:])

        def quantize_xq0(h):
            quantize(xq_c[0][:, h * half : (h + 1) * half], xq_s[0][:, h * half : (h + 1) * half], grp0[h][:])

        def precision_b(k):
            softplus(pb[k], dealt(bank_v[k]), lv[k])

        for h in range(2):
            round_xq0(h)
            quantize_xq0(h)
        for k in range(TILES):
            log_of(lv[k], ev[k])

        def estimate_b(k):
            precision_b(k)
            for z in range(PASSES):
                xq_pass(bank_v[k], k, z, wq_w, wq_s)

        for h in range(2):
            for k in (2 * h, 2 * h + 1):
                round_xq1(k)
            for k in (2 * h, 2 * h + 1):
                quantize_xq1(k)
        for k in range(TILES):
            for z in range(PASSES):
                xq_pass(bank_u[k], k, z, va_w, va_s)
            exp_of(eu[k], bank_u[k])
            if k > 0:
                estimate_b(k - 1)
        estimate_b(TILES - 1)
        def product_b(k):
            product(tb[k], bank_v[k], pb[k])
            transpose_into(bank_v[k], pb[k], True, False)

        def keep_u(k):
            nc.vector.tensor_copy(out=u_sb[k][:], in_=dealt(bank_u[k]))

        def estimate_a(k):
            for z in range(PASSES):
                xt_pass(bank_u[k], k, z, wa_w, wa_s)

        for k in range(TILES):
            product_b(k)
            keep_u(k)
            if k < 2:
                estimate_a(k)
            log_of(lu[k], eu[k])

        def reciprocal_root(k):
            nc.scalar.activation(
                out=root[k][:], in_=by_r(bank_v[k]), func=ACT.Abs_reciprocal_sqrt, scale=10.0, bias=ones[:]
            )

        def square(k):
            if k < 2:
                engine = nc.vector if k == 0 else nc.gpsimd
                engine.tensor_tensor(out=recip[k][:], in0=root[k][:], in1=root[k][:], op=ALU.mult)
            else:
                nc.scalar.activation(out=recip[k][:], in_=root[k][:], func=ACT.Square)

        out_rows = out_0.rearrange("(p r) t -> p r t", r=PACK)
        out_words = out_1[0].rearrange("p c r -> p (c r)").bitcast(I32)

        def result(k):
            nc.vector.scalar_tensor_tensor(
                out=y[k][:].rearrange("p r t -> p (r t)"), in0=bank_u[k][:], scalar=10.0,
                in1=recip[k][:].rearrange("p r t -> p (r t)"), op0=ALU.mult, op1=ALU.mult,
            )
            nc.sync.dma_start(out=out_rows[:, :, cols(k)], in_=y[k][:])

        def round_result(k):
            interleave(nc.scalar.copy if k < 3 else nc.vector.tensor_copy, y_grp[k][:], y[k][:])

        def planes(k):
            quantize(y_c[:, cols(k)], y_s[:, cols(k)], y_grp[k][:])

        def store_words(span):
            nc.sync.dma_start(out=out_words[:, span], in_=y_c[:, span].bitcast(I32))

        def precision_a(k):
            softplus(pa[k], u_sb[k][:], lu[k])
            transpose_into(bank_v[k], pa[k], False, True)

        def numerator(k):
            product(ta[k], bank_u[k], pa[k])
            transpose_into(bank_u[k], tb[k], True, False)
            transpose_into(bank_u[k], ta[k], False, True)

        estimate_a(2)
        precision_a(0)
        precision_a(1)
        numerator(0)
        estimate_a(3)
        precision_a(2)
        precision_a(3)
        numerator(1)
        numerator(2)
        for k in range(TILES):
            reciprocal_root(k)
        for k in range(TILES):
            square(k)
        numerator(3)
        for k in range(TILES - 1):
            result(k)
            round_result(k)
        result(3)
        planes(0)
        planes(1)
        store_words(slice(0, half))
        round_result(3)
        planes(2)
        planes(3)
        store_words(slice(half, T))
        for q in range(4):
            nc.scalar.dma_start(
                out=out_2[0, 4 * q : 4 * q + 4, :].bitcast(I32), in_=y_s[32 * q : 32 * q + 4, :].bitcast(I32)
            )
